import numpy as np
import ml_dtypes


def mxq(x, axis, fmt="e4m3"):
    dtype, down = {"e4m3": (ml_dtypes.float8_e4m3fn, 7), "e5m2": (ml_dtypes.float8_e5m2, 14)}[fmt]
    v = np.moveaxis(np.asarray(x, np.float32).astype(ml_dtypes.bfloat16).astype(np.float64), axis, -1)
    blocks = v.reshape(v.shape[:-1] + (-1, 32))
    amax = np.abs(blocks).max(-1, keepdims=True)
    byte = np.maximum(np.where(amax > 0, np.frexp(amax)[1] - 1 + 127, 0) - down, 1)
    scale = np.exp2(byte - 127.0)
    codes = (blocks / scale).astype(np.float32).astype(dtype).astype(np.float64)
    return np.moveaxis((codes * scale).reshape(v.shape), -1, axis)


WIDE = False


def mx_kscale(k):
    if not WIDE:
        return np.ones(k)
    levels = np.array([10, -10, 5, -5, 0])
    if k % 512:
        return np.exp2(np.random.permutation(np.resize(levels, k // 32))).repeat(32)
    a = np.empty((k // 512, 16))
    for p in range(k // 512):
        a[p, :8] = np.random.permutation(np.resize(levels, 8))
        for g in range(8):
            far = levels[np.abs(levels - a[p, g]) >= 10]
            a[p, g + 8] = far[np.random.randint(len(far))]
    return np.exp2(a.ravel()).repeat(32)


BF16 = ml_dtypes.bfloat16


def bf(x):
    return np.asarray(x, np.float32).astype(BF16)


def f64(x):
    return np.asarray(x).astype(np.float64)

def planes(Y):
    n, m = Y.shape
    b = f64(bf(Y)).reshape(n // 32, 32, m)
    amax = np.abs(b).max(1)
    byte = np.clip(np.where(amax > 0, np.frexp(amax)[1] - 1 + 127 - 7, 1), 1, 254)
    codes = (b * np.exp2(127.0 - byte)[:, None, :]).reshape(n, m).astype(np.float32).astype(ml_dtypes.float8_e4m3fn).view(np.uint8)
    words = codes.reshape(n // 512, 128, 4, m).transpose(0, 1, 3, 2)
    return np.ascontiguousarray(words), np.ascontiguousarray(byte.astype(np.uint8).reshape(n // 512, 16, m))


N, J, P, H, C, O = 1024, 4, 3, 512, 512, 512
JC = J * C

SLOPE = 0.2


def setup_inputs():
    t, u = mx_kscale(H), mx_kscale(JC)
    return {
        "rel": bf(np.random.standard_normal((N, J, P))),
        "w1": bf(np.random.standard_normal((P, H)) / np.sqrt(P) * t),
        "b1": bf(np.random.standard_normal(H) * 0.4 * t),
        "w2": bf(np.random.standard_normal((H, C)) / np.sqrt(H) / t[:, None]),
        "b2": bf(np.random.standard_normal(C) * 0.4),
        "f": bf(np.random.standard_normal((N, J, C)) * u.reshape(J, C)),
        "wo": bf(np.random.standard_normal((J, C, O)) / np.sqrt(JC) / u.reshape(J, C, 1)),
    }


def _offset_layer(rel, w1, b1):
    a = rel[:, :, 0, None] * w1[0]
    for i in range(1, w1.shape[0]):
        a = a + rel[:, :, i, None] * w1[i]
    return a + b1


def _leaky(a):
    return np.where(a > 0, a, SLOPE * a)


def core(rel, w1, b1, w2, b2, f, wo):
    rel, w1, b1, w2, b2, f, wo = f64(rel), f64(w1), f64(b1), f64(w2), f64(b2), f64(f), f64(wo)
    n, j, c = f.shape
    o = wo.shape[-1]
    a = _offset_layer(rel, w1, b1)
    m = _leaky(a)
    k = (mxq(m, 2, "e4m3") @ mxq(w2, 0, "e4m3")) + b2
    p = k * f
    return mxq(p.reshape(n, j * c), 1, "e4m3") @ mxq(wo.reshape(j * c, o), 0, "e4m3")


def reference(rel, w1, b1, w2, b2, f, wo):
    R_out = core(rel, w1, b1, w2, b2, f, wo)
    words, scales = planes(R_out.T)
    return R_out, words, scales

@@ -1,0 +1,274 @@
+from contextlib import ExitStack
+
+import concourse.mybir as mybir
+from concourse.masks import make_identity
+
+F32 = mybir.dt.float32
+BF16 = mybir.dt.bfloat16
+U32 = mybir.dt.uint32
+I32 = mybir.dt.int32
+U8 = mybir.dt.uint8
+FP8X4 = mybir.dt.float8_e4m3fn_x4
+ALU = mybir.AluOpType
+ACT = mybir.ActivationFunctionType
+
+N, J, H, C, O = 1024, 4, 512, 512, 512
+FLOPS = 2 * N * J * H * C + 2 * N * J * C * O
+ROWS = 256
+NT = N // ROWS
+UNITS = NT * J
+SLOPE = 0.2
+
+
+def tile_rangeviewmetakernelfourneighbour_x1_kernel(tc, rel, w1, b1, w2, b2, f, wo, out_0, out_1, out_2):
+    nc = tc.nc
+    with ExitStack() as ctx:
+        keep = ctx.enter_context(tc.tile_pool(name="keep", bufs=1))
+        work = ctx.enter_context(tc.tile_pool(name="work", bufs=2))
+        psum = ctx.enter_context(tc.psum_pool(name="psum", bufs=1))
+        ctx.enter_context(tc.manual_schedule())
+
+        b1_raw = keep.tile([128, 4], BF16, name="b1_raw")
+        nc.sync.dma_start(out=b1_raw[:], in_=b1.rearrange("(p t) -> p t", t=4))
+        b2_raw = keep.tile([128, 4], BF16, name="b2_raw")
+        nc.sync.dma_start(out=b2_raw[:], in_=b2.rearrange("(p t) -> p t", t=4))
+        rel_raw = keep.tile([128, 8, 12], BF16, name="rel_raw")
+        nc.sync.dma_start(out=rel_raw[:], in_=rel.rearrange("(a p) j i -> p a (j i)", p=128))
+        w1_raw = keep.tile([128, 3, 512], BF16, name="w1_raw")
+        nc.sync.dma_start(out=w1_raw[:], in_=w1.partition_broadcast(128))
+        w2_raw = keep.tile([128, 4, 512], BF16, name="w2_raw")
+        nc.sync.dma_start(out=w2_raw[:], in_=w2.rearrange("(p k) c -> p k c", k=4))
+        wo_raw = [keep.tile([128, 4, 512], BF16, name=f"wo_raw{j}") for j in range(J)]
+        f_sb = [keep.tile([128, J, 512], BF16, name=f"f_sb{a}") for a in range(8)]
+
+        def load_wo(j):
+            nc.sync.dma_start(out=wo_raw[j][:], in_=wo[j].rearrange("(p k) c -> p k c", k=4))
+
+        def load_f(a):
+            nc.sync.dma_start(out=f_sb[a][:], in_=f[a * 128 : (a + 1) * 128])
+
+        load_wo(0)
+        load_f(0)
+        load_f(1)
+        load_wo(2)
+        load_wo(1)
+        load_wo(3)
+        for a in range(2, 8):
+            load_f(a)
+
+        ident = keep.tile([128, 128], F32, name="ident")
+        make_identity(nc, ident[:])
+
+        b1c = keep.tile([128, 4], F32, name="b1c")
+        b2c = keep.tile([128, 4], F32, name="b2c")
+        nc.scalar.activation(b1c[:], b1_raw[:], ACT.Identity)
+        nc.scalar.activation(b2c[:], b2_raw[:], ACT.Identity)
+        relf = keep.tile([128, 8, 12], F32, name="relf")
+        nc.vector.tensor_copy(out=relf[:], in_=rel_raw[:])
+        w1p = keep.tile([128, 3, 4, 128], BF16, name="w1p")
+        for i in range(3):
+            nc.vector.tensor_copy(out=w1p[:, i, :, :], in_=w1_raw[:, i, :].rearrange("p (q t) -> p t q", t=4))
+
+        w2_q = keep.tile([128, 512], U32, name="w2_q", align_bytes=64)
+        w2_s = keep.tile([128, 512], U8, name="w2_s", align_bytes=64)
+        wo_q = [keep.tile([128, 512], U32, name=f"wo_q{j}", align_bytes=64) for j in range(J)]
+        wo_s = [keep.tile([128, 512], U8, name=f"wo_s{j}", align_bytes=64) for j in range(J)]
+        w_grp = {}
+
+        def interleave(key, raw, eng):
+            g = work.tile([128, 2048], BF16, name="w_grp", align_bytes=64, bufs=3)
+            w_grp[key] = g
+            dst = g[:].rearrange("p (t m k) -> p t m k", t=4, k=4)
+            src = raw[:].rearrange("p k (m t) -> p t m k", t=4)
+            for t in range(4):
+                if eng == "v":
+                    nc.vector.tensor_copy(out=dst[:, t], in_=src[:, t])
+                else:
+                    nc.scalar.copy(dst[:, t], src[:, t])
+
+        def quant_w(key, q, s):
+            nc.vector.quantize_mx(out=q[:].bitcast(FP8X4), scales=s[:], in_=w_grp[key][:])
+
+        prods, a_ps, a_sb, m_bf, m_q, k_ps, k_sb, f_ps, p_bf = {}, {}, {}, {}, {}, {}, {}, {}, {}
+        p_q = {}
+        S_PROD = ((0, 2), (1, 2))
+
+        def alloc_prod(u):
+            prods[u] = [work.tile([128, 3, 512], F32, name=f"prod{h}", align_bytes=64) for h in range(2)]
+
+        def prod(u, h, i):
+            g, j = divmod(u, J)
+            col = relf[:, 2 * g + h, 3 * j + i : 3 * j + i + 1]
+            src = w1p[:, i].rearrange("p t q -> p (t q)")
+            if (h, i) in S_PROD:
+                nc.scalar.activation(prods[u][h][:, i, :], src, ACT.Identity, scale=col)
+            else:
+                nc.vector.tensor_scalar(out=prods[u][h][:, i, :], in0=src, scalar1=col, scalar2=None, op0=ALU.mult)
+
+        def tr_a(u):
+            a_ps[u] = []
+            for tp in range(2):
+                bank = psum.tile([128, 2, ROWS], F32, name=f"a_ps{tp}")
+                a_ps[u].append(bank)
+                for h in range(2):
+                    for tl in range(2):
+                        t = 2 * tp + tl
+                        for i in range(3):
+                            nc.tensor.matmul(bank[:, tl, h * 128 : (h + 1) * 128], lhsT=prods[u][h][:, i, t * 128 : (t + 1) * 128], rhs=ident[:], start=(i == 0), stop=(i == 2), is_transpose=True)
+
+        def rd_a(u):
+            a_sb[u] = work.tile([128, 4, ROWS], F32, name="a_sb", align_bytes=64)
+            for t in range(4):
+                nc.scalar.activation(a_sb[u][:, t, :], a_ps[u][t // 2][:, t % 2, :], ACT.Identity, bias=b1c[:, t : t + 1])
+
+        def leaky(u):
+            m_bf[u] = work.tile([128, ROWS, 4], BF16, name="m_bf", align_bytes=64)
+            a = a_sb[u][:].rearrange("p t r -> p r t")
+            nc.vector.scalar_tensor_tensor(out=m_bf[u][:], in0=a, scalar=SLOPE, in1=a, op0=ALU.mult, op1=ALU.max)
+
+        def quant_m(u):
+            m_q[u] = (work.tile([128, ROWS], U32, name="m_q", align_bytes=64), work.tile([128, ROWS], U8, name="m_s", align_bytes=64))
+            nc.vector.quantize_mx(out=m_q[u][0][:].bitcast(FP8X4), scales=m_q[u][1][:], in_=m_bf[u][:].rearrange("p r t -> p (r t)"))
+
+        def mx1(u):
+            k_ps[u] = []
+            for tp in range(2):
+                bank = psum.tile([128, 2, ROWS], F32, name=f"k_ps{tp}")
+                k_ps[u].append(bank)
+                for tl in range(2):
+                    cols = slice((2 * tp + tl) * 128, (2 * tp + tl + 1) * 128)
+                    nc.tensor.matmul_mx(bank[:, tl, :], lhsT=w2_q[:, cols].bitcast(FP8X4), lhsT_scale=w2_s[:, cols], rhs=m_q[u][0][:].bitcast(FP8X4), rhs_scale=m_q[u][1][:], start=True, stop=True)
+
+        def rd_k(u):
+            k_sb[u] = work.tile([128, 4, ROWS], F32, name="k_sb", align_bytes=64)
+            for t in range(4):
+                nc.scalar.activation(k_sb[u][:, t, :], k_ps[u][t // 2][:, t % 2, :], ACT.Identity, bias=b2c[:, t : t + 1])
+
+        def tr_f(u):
+            g, j = divmod(u, J)
+            f_ps[u] = psum.tile([128, 2, ROWS], F32, name="f_ps", bufs=2)
+            for h in range(2):
+                words = f_sb[2 * g + h][:, j, :].bitcast(F32)
+                for e in range(2):
+                    nc.tensor.transpose(f_ps[u][:, e, h * 128 : (h + 1) * 128], words[:, e : 256 : 2], ident[:])
+
+        def times_f(u):
+            p_bf[u] = work.tile([128, ROWS, 4], BF16, name="p_bf", align_bytes=64)
+            fv = f_ps[u][:].rearrange("p u n -> p (u n)").bitcast(BF16).rearrange("p (u n e) -> p n u e", u=2, e=2)
+            kv = k_sb[u][:].rearrange("p (u e) n -> p n u e", e=2)
+            nc.vector.tensor_tensor(out=p_bf[u][:].rearrange("p n (u e) -> p n u e", e=2), in0=fv, in1=kv, op=ALU.mult)
+
+        def quant_p(u):
+            g, j = divmod(u, J)
+            if j == 0:
+                p_q[g] = (work.tile([128, J, ROWS], U32, name="p_q", align_bytes=64), work.tile([128, J, ROWS], U8, name="p_s", align_bytes=64))
+            nc.vector.quantize_mx(out=p_q[g][0][:, j, :].bitcast(FP8X4), scales=p_q[g][1][:, j, :], in_=p_bf[u][:].rearrange("p n t -> p (n t)"))
+
+        o_ps, o_sb, o_bf, t_ps = {}, {}, {}, {}
+        o_q = keep.tile([128, N], U32, name="o_q", align_bytes=64)
+        o_s = keep.tile([128, N], U8, name="o_s", align_bytes=64)
+
+        def mx2(a):
+            g, h = divmod(a, 2)
+            o_ps[a] = psum.tile([128, 4, 128], F32, name="o_ps", bufs=2)
+            rows = slice(h * 128, (h + 1) * 128)
+            for t in range(4):
+                cols = slice(t * 128, (t + 1) * 128)
+                for j in range(J):
+                    nc.tensor.matmul_mx(o_ps[a][:, t, :], lhsT=wo_q[j][:, cols].bitcast(FP8X4), lhsT_scale=wo_s[j][:, cols], rhs=p_q[g][0][:, j, rows].bitcast(FP8X4), rhs_scale=p_q[g][1][:, j, rows], start=(j == 0), stop=(j == J - 1))
+
+        def rd_o(a):
+            o_sb[a] = work.tile([128, 4, 128], F32, name="o_sb", align_bytes=64)
+            nc.scalar.activation(o_sb[a][:], o_ps[a][:], ACT.Identity)
+
+        def group_o(a):
+            o_bf[a] = work.tile([128, 128, 4], BF16, name="o_bf", align_bytes=64)
+            nc.vector.tensor_copy(out=o_bf[a][:], in_=o_sb[a][:].rearrange("p t n -> p n t"))
+
+        def quant_o(a):
+            cols = slice(a * 128, (a + 1) * 128)
+            nc.vector.quantize_mx(out=o_q[:, cols].bitcast(FP8X4), scales=o_s[:, cols], in_=o_bf[a][:].rearrange("p n t -> p (n t)"))
+            nc.sync.dma_start(out=out_1[0, :, cols, :].rearrange("p m t -> p (m t)").bitcast(I32), in_=o_q[:, cols].bitcast(I32))
+
+        def store_scales(c0, c1):
+            for q in range(4):
+                nc.sync.dma_start(out=out_2[0, 4 * q : 4 * q + 4, c0:c1].bitcast(I32), in_=o_s[32 * q : 32 * q + 4, c0:c1].bitcast(I32))
+
+        def tr_o(a):
+            t_ps[a] = psum.tile([128, 4, 128], F32, name="o_ps", bufs=2)
+            for t in range(4):
+                nc.tensor.transpose(t_ps[a][:, t, :], o_sb[a][:, t, :], ident[:])
+
+        def rd_t(a, eng):
+            r = work.tile([128, 128, 4], F32, name="r_sb", align_bytes=64)
+            src = t_ps[a][:].rearrange("n t m -> n m t")
+            if eng == "v":
+                nc.vector.tensor_copy(out=r[:], in_=src)
+            else:
+                nc.scalar.activation(r[:], src, ACT.Identity)
+            nc.sync.dma_start(out=out_0[a * 128 : (a + 1) * 128, :], in_=r[:].rearrange("n m t -> n (m t)"))
+
+        fill = {}
+        for g in range(NT - 1):
+            fill[4 * g + 7] = [2 * g]
+            fill[4 * g + 9] = [2 * g + 1]
+        fill[19] = [6, 7]
+
+        ok = lambda u: 0 <= u < UNITS
+        for s in range(22):
+            outs1 = fill.get(s - 1, [])
+            outs2 = fill.get(s - 2, [])
+            if ok(s - 3):
+                rd_k(s - 3)
+            for a in outs1:
+                rd_o(a)
+            if ok(s - 2):
+                leaky(s - 2)
+            if ok(s):
+                alloc_prod(s)
+                for i in range(3):
+                    prod(s, 0, i)
+            if ok(s - 2):
+                quant_m(s - 2)
+            if ok(s - 1):
+                tr_a(s - 1)
+            for a in outs2:
+                tr_o(a)
+            if ok(s - 2):
+                tr_f(s - 2)
+                mx1(s - 2)
+            for a in fill.get(s, []):
+                mx2(a)
+            if ok(s):
+                for i in range(3):
+                    prod(s, 1, i)
+            if ok(s - 3):
+                times_f(s - 3)
+            for a in outs1:
+                group_o(a)
+            if ok(s - 1):
+                rd_a(s - 1)
+            if ok(s - 3):
+                quant_p(s - 3)
+            for a in outs1:
+                quant_o(a)
+            for a in outs2:
+                rd_t(a, "s" if a != 7 else "v")
+            if s == 0:
+                interleave("w2", w2_raw, "v")
+                quant_w("w2", w2_q, w2_s)
+            if s == 1:
+                interleave(0, wo_raw[0], "s")
+                interleave(2, wo_raw[2], "v")
+            if s == 2:
+                quant_w(0, wo_q[0], wo_s[0])
+                quant_w(2, wo_q[2], wo_s[2])
+                interleave(1, wo_raw[1], "s")
+                interleave(3, wo_raw[3], "v")
+            if s == 3:
+                quant_w(1, wo_q[1], wo_s[1])
+                quant_w(3, wo_q[3], wo_s[3])
+            if s == 18:
+                store_scales(0, 768)
+            if s == 20:
+                store_scales(768, 1024)

@@ -91,7 +91,8 @@ def tile_rangeviewmetakernelfourneighbour_x1_kernel(tc, rel, w1, b1, w2, b2, f, 
 
         prods, a_ps, a_sb, m_bf, m_q, k_ps, k_sb, f_ps, p_bf = {}, {}, {}, {}, {}, {}, {}, {}, {}
         p_q = {}
-        S_PROD = ((0, 2), (1, 2))
+        PASSES = ((0, 1, 2), (1, 2))
+        S_PROD = ((0, 0), (0, 2), (1, 0))
 
         def alloc_prod(u):
             prods[u] = [work.tile([128, 3, 512], F32, name=f"prod{h}", align_bytes=64) for h in range(2)]
@@ -102,19 +103,19 @@ def tile_rangeviewmetakernelfourneighbour_x1_kernel(tc, rel, w1, b1, w2, b2, f, 
             src = w1p[:, i].rearrange("p t q -> p (t q)")
             if (h, i) in S_PROD:
                 nc.scalar.activation(prods[u][h][:, i, :], src, ACT.Identity, scale=col)
-            else:
+            elif i not in PASSES[h] or i - 1 in PASSES[h] or i == 0:
                 nc.vector.tensor_scalar(out=prods[u][h][:, i, :], in0=src, scalar1=col, scalar2=None, op0=ALU.mult)
+            else:
+                nc.vector.scalar_tensor_tensor(out=prods[u][h][:, i, :], in0=src, scalar=col, in1=prods[u][h][:, i - 1, :], op0=ALU.mult, op1=ALU.add)
 
-        def tr_a(u):
-            a_ps[u] = []
-            for tp in range(2):
-                bank = psum.tile([128, 2, ROWS], F32, name=f"a_ps{tp}")
-                a_ps[u].append(bank)
-                for h in range(2):
-                    for tl in range(2):
-                        t = 2 * tp + tl
-                        for i in range(3):
-                            nc.tensor.matmul(bank[:, tl, h * 128 : (h + 1) * 128], lhsT=prods[u][h][:, i, t * 128 : (t + 1) * 128], rhs=ident[:], start=(i == 0), stop=(i == 2), is_transpose=True)
+        def tr_a(u, tp):
+            bank = psum.tile([128, 2, ROWS], F32, name=f"a_ps{tp}")
+            a_ps.setdefault(u, []).append(bank)
+            for h in range(2):
+                for tl in range(2):
+                    t = 2 * tp + tl
+                    for i in PASSES[h]:
+                        nc.tensor.matmul(bank[:, tl, h * 128 : (h + 1) * 128], lhsT=prods[u][h][:, i, t * 128 : (t + 1) * 128], rhs=ident[:], start=(i == PASSES[h][0]), stop=(i == 2), is_transpose=True)
 
         def rd_a(u):
             a_sb[u] = work.tile([128, 4, ROWS], F32, name="a_sb", align_bytes=64)
@@ -164,26 +165,31 @@ def tile_rangeviewmetakernelfourneighbour_x1_kernel(tc, rel, w1, b1, w2, b2, f, 
                 p_q[g] = (work.tile([128, J, ROWS], U32, name="p_q", align_bytes=64), work.tile([128, J, ROWS], U8, name="p_s", align_bytes=64))
             nc.vector.quantize_mx(out=p_q[g][0][:, j, :].bitcast(FP8X4), scales=p_q[g][1][:, j, :], in_=p_bf[u][:].rearrange("p n t -> p (n t)"))
 
-        o_ps, o_sb, o_bf, t_ps = {}, {}, {}, {}
+        o_ps, o_bf, t_ps = {}, {}, {}
         o_q = keep.tile([128, N], U32, name="o_q", align_bytes=64)
         o_s = keep.tile([128, N], U8, name="o_s", align_bytes=64)
 
-        def mx2(a):
+        def mx2_planes(a, part):
             g, h = divmod(a, 2)
-            o_ps[a] = psum.tile([128, 4, 128], F32, name="o_ps", bufs=2)
+            if part == 0:
+                o_ps[a] = psum.tile([128, 4, 128], F32, name="o_ps", bufs=2)
             rows = slice(h * 128, (h + 1) * 128)
-            for t in range(4):
+            for t in (0, 1) if part == 0 else (2, 3):
                 cols = slice(t * 128, (t + 1) * 128)
                 for j in range(J):
                     nc.tensor.matmul_mx(o_ps[a][:, t, :], lhsT=wo_q[j][:, cols].bitcast(FP8X4), lhsT_scale=wo_s[j][:, cols], rhs=p_q[g][0][:, j, rows].bitcast(FP8X4), rhs_scale=p_q[g][1][:, j, rows], start=(j == 0), stop=(j == J - 1))
 
-        def rd_o(a):
-            o_sb[a] = work.tile([128, 4, 128], F32, name="o_sb", align_bytes=64)
-            nc.scalar.activation(o_sb[a][:], o_ps[a][:], ACT.Identity)
+        def mx2_rows(a, part):
+            g, h = divmod(a, 2)
+            if part == 0:
+                t_ps[a] = psum.tile([128, 4, 128], F32, name="o_ps", bufs=2)
+            rows = slice(h * 128, (h + 1) * 128)
+            for j in (0, 1) if part == 0 else (2, 3):
+                nc.tensor.matmul_mx(t_ps[a][:].rearrange("n t m -> n (t m)"), lhsT=p_q[g][0][:, j, rows].bitcast(FP8X4), lhsT_scale=p_q[g][1][:, j, rows], rhs=wo_q[j][:].bitcast(FP8X4), rhs_scale=wo_s[j][:], start=(j == 0), stop=(j == J - 1))
 
         def group_o(a):
             o_bf[a] = work.tile([128, 128, 4], BF16, name="o_bf", align_bytes=64)
-            nc.vector.tensor_copy(out=o_bf[a][:], in_=o_sb[a][:].rearrange("p t n -> p n t"))
+            nc.vector.tensor_copy(out=o_bf[a][:], in_=o_ps[a][:].rearrange("p t n -> p n t"))
 
         def quant_o(a):
             cols = slice(a * 128, (a + 1) * 128)
@@ -193,11 +199,6 @@ def tile_rangeviewmetakernelfourneighbour_x1_kernel(tc, rel, w1, b1, w2, b2, f, 
         def store_scales(c0, c1):
             for q in range(4):
                 nc.sync.dma_start(out=out_2[0, 4 * q : 4 * q + 4, c0:c1].bitcast(I32), in_=o_s[32 * q : 32 * q + 4, c0:c1].bitcast(I32))
-
-        def tr_o(a):
-            t_ps[a] = psum.tile([128, 4, 128], F32, name="o_ps", bufs=2)
-            for t in range(4):
-                nc.tensor.transpose(t_ps[a][:, t, :], o_sb[a][:, t, :], ident[:])
 
         def rd_t(a, eng):
             r = work.tile([128, 128, 4], F32, name="r_sb", align_bytes=64)
@@ -209,51 +210,55 @@ def tile_rangeviewmetakernelfourneighbour_x1_kernel(tc, rel, w1, b1, w2, b2, f, 
             nc.sync.dma_start(out=out_0[a * 128 : (a + 1) * 128, :], in_=r[:].rearrange("n m t -> n (m t)"))
 
         fill = {}
-        for g in range(NT - 1):
-            fill[4 * g + 7] = [2 * g]
-            fill[4 * g + 9] = [2 * g + 1]
-        fill[19] = [6, 7]
+        for q in range(8):
+            g, h = divmod(q, 2)
+            fill[4 * g + 7 + 2 * h] = [("p", q)]
+            fill[4 * g + 8 + 2 * h] = [("r", q)]
+        fill[19], fill[20], fill[21], fill[22] = [("p", 6), ("p", 7)], [("r", 6), ("r", 7)], [], []
 
         ok = lambda u: 0 <= u < UNITS
+        mx2 = lambda kq, part: mx2_planes(kq[1], part) if kq[0] == "p" else mx2_rows(kq[1], part)
         for s in range(22):
-            outs1 = fill.get(s - 1, [])
-            outs2 = fill.get(s - 2, [])
+            now = fill.get(s, [])
+            planes = [q for k, q in fill.get(s - 1, []) if k == "p"]
+            rows = [q for k, q in fill.get(s - 1, []) if k == "r"]
             if ok(s - 3):
                 rd_k(s - 3)
-            for a in outs1:
-                rd_o(a)
+            for q in rows:
+                rd_t(q, "s" if q != 7 else "v")
             if ok(s - 2):
                 leaky(s - 2)
             if ok(s):
                 alloc_prod(s)
+                prod(s, 1, 0)
                 for i in range(3):
                     prod(s, 0, i)
             if ok(s - 2):
                 quant_m(s - 2)
             if ok(s - 1):
-                tr_a(s - 1)
-            for a in outs2:
-                tr_o(a)
+                tr_a(s - 1, 0)
+            for q in now:
+                mx2(q, 0)
+            if ok(s - 1):
+                tr_a(s - 1, 1)
             if ok(s - 2):
                 tr_f(s - 2)
                 mx1(s - 2)
-            for a in fill.get(s, []):
-                mx2(a)
+            for q in now:
+                mx2(q, 1)
             if ok(s):
-                for i in range(3):
-                    prod(s, 1, i)
+                prod(s, 1, 1)
+                prod(s, 1, 2)
             if ok(s - 3):
                 times_f(s - 3)
-            for a in outs1:
-                group_o(a)
+            for q in planes:
+                group_o(q)
             if ok(s - 1):
                 rd_a(s - 1)
             if ok(s - 3):
                 quant_p(s - 3)
-            for a in outs1:
-                quant_o(a)
-            for a in outs2:
-                rd_t(a, "s" if a != 7 else "v")
+            for q in planes:
+                quant_o(q)
             if s == 0:
                 interleave("w2", w2_raw, "v")
                 quant_w("w2", w2_q, w2_s)

@@ -14,9 +14,8 @@ ACT = mybir.ActivationFunctionType
 
 N, J, H, C, O = 1024, 4, 512, 512, 512
 FLOPS = 2 * N * J * H * C + 2 * N * J * C * O
-ROWS = 256
-NT = N // ROWS
-UNITS = NT * J
+GROUPS = [(0, 256), (256, 256), (512, 256), (768, 256)]
+UNITS = [(g, j) for g in range(len(GROUPS)) for j in range(J)]
 SLOPE = 0.2
 
 
@@ -28,18 +27,24 @@ def tile_rangeviewmetakernelfourneighbour_x1_kernel(tc, rel, w1, b1, w2, b2, f, 
         psum = ctx.enter_context(tc.psum_pool(name="psum", bufs=1))
         ctx.enter_context(tc.manual_schedule())
 
-        b1_raw = keep.tile([128, 4], BF16, name="b1_raw")
-        nc.sync.dma_start(out=b1_raw[:], in_=b1.rearrange("(p t) -> p t", t=4))
-        b2_raw = keep.tile([128, 4], BF16, name="b2_raw")
-        nc.sync.dma_start(out=b2_raw[:], in_=b2.rearrange("(p t) -> p t", t=4))
-        rel_raw = keep.tile([128, 8, 12], BF16, name="rel_raw")
-        nc.sync.dma_start(out=rel_raw[:], in_=rel.rearrange("(a p) j i -> p a (j i)", p=128))
-        w1_raw = keep.tile([128, 3, 512], BF16, name="w1_raw")
-        nc.sync.dma_start(out=w1_raw[:], in_=w1.partition_broadcast(128))
         w2_raw = keep.tile([128, 4, 512], BF16, name="w2_raw")
-        nc.sync.dma_start(out=w2_raw[:], in_=w2.rearrange("(p k) c -> p k c", k=4))
+        rel_raw = keep.tile([128, 8, 12], BF16, name="rel_raw")
+        w1_raw = keep.tile([128, 3, 512], BF16, name="w1_raw")
+        b1_raw = keep.tile([128, 4], BF16, name="b1_raw")
+        b2_raw = keep.tile([128, 4], BF16, name="b2_raw")
         wo_raw = [keep.tile([128, 4, 512], BF16, name=f"wo_raw{j}") for j in range(J)]
         f_sb = [keep.tile([128, J, 512], BF16, name=f"f_sb{a}") for a in range(8)]
+
+        def load_w2():
+            nc.sync.dma_start(out=w2_raw[:], in_=w2.rearrange("(p k) c -> p k c", k=4))
+
+        def load_rel():
+            nc.sync.dma_start(out=rel_raw[:], in_=rel.rearrange("(a p) j i -> p a (j i)", p=128))
+            nc.sync.dma_start(out=b1_raw[:], in_=b1.rearrange("(p t) -> p t", t=4))
+            nc.sync.dma_start(out=b2_raw[:], in_=b2.rearrange("(p t) -> p t", t=4))
+
+        def load_w1():
+            nc.sync.dma_start(out=w1_raw[:], in_=w1.partition_broadcast(128))
 
         def load_wo(j):
             nc.sync.dma_start(out=wo_raw[j][:], in_=wo[j].rearrange("(p k) c -> p k c", k=4))
@@ -47,11 +52,14 @@ def tile_rangeviewmetakernelfourneighbour_x1_kernel(tc, rel, w1, b1, w2, b2, f, 
         def load_f(a):
             nc.sync.dma_start(out=f_sb[a][:], in_=f[a * 128 : (a + 1) * 128])
 
+        load_w2()
         load_wo(0)
+        load_rel()
+        load_w1()
+        load_wo(1)
+        load_wo(2)
         load_f(0)
         load_f(1)
-        load_wo(2)
-        load_wo(1)
         load_wo(3)
         for a in range(2, 8):
             load_f(a)
@@ -61,13 +69,15 @@ def tile_rangeviewmetakernelfourneighbour_x1_kernel(tc, rel, w1, b1, w2, b2, f, 
 
         b1c = keep.tile([128, 4], F32, name="b1c")
         b2c = keep.tile([128, 4], F32, name="b2c")
-        nc.scalar.activation(b1c[:], b1_raw[:], ACT.Identity)
-        nc.scalar.activation(b2c[:], b2_raw[:], ACT.Identity)
         relf = keep.tile([128, 8, 12], F32, name="relf")
-        nc.vector.tensor_copy(out=relf[:], in_=rel_raw[:])
         w1p = keep.tile([128, 3, 4, 128], BF16, name="w1p")
-        for i in range(3):
-            nc.vector.tensor_copy(out=w1p[:, i, :, :], in_=w1_raw[:, i, :].rearrange("p (q t) -> p t q", t=4))
+
+        def permute(eng, i):
+            v = w1_raw[:, i, :].rearrange("p (q t) -> p t q", t=4)
+            if eng == "v":
+                nc.vector.tensor_copy(out=w1p[:, i], in_=v)
+            else:
+                nc.scalar.copy(w1p[:, i], v)
 
         w2_q = keep.tile([128, 512], U32, name="w2_q", align_bytes=64)
         w2_s = keep.tile([128, 512], U8, name="w2_s", align_bytes=64)
@@ -75,132 +85,157 @@ def tile_rangeviewmetakernelfourneighbour_x1_kernel(tc, rel, w1, b1, w2, b2, f, 
         wo_s = [keep.tile([128, 512], U8, name=f"wo_s{j}", align_bytes=64) for j in range(J)]
         w_grp = {}
 
-        def interleave(key, raw, eng):
-            g = work.tile([128, 2048], BF16, name="w_grp", align_bytes=64, bufs=3)
-            w_grp[key] = g
-            dst = g[:].rearrange("p (t m k) -> p t m k", t=4, k=4)
+        def interleave(key, raw, on_scalar, parts=(0, 1, 2, 3)):
+            if key not in w_grp:
+                w_grp[key] = work.tile([128, 2048], BF16, name="w_grp", align_bytes=64, bufs=4)
+            dst = w_grp[key][:].rearrange("p (t m k) -> p t m k", t=4, k=4)
             src = raw[:].rearrange("p k (m t) -> p t m k", t=4)
-            for t in range(4):
-                if eng == "v":
-                    nc.vector.tensor_copy(out=dst[:, t], in_=src[:, t])
-                else:
+            for t in parts:
+                if t in on_scalar:
                     nc.scalar.copy(dst[:, t], src[:, t])
+                else:
+                    nc.vector.tensor_copy(out=dst[:, t], in_=src[:, t])
 
         def quant_w(key, q, s):
             nc.vector.quantize_mx(out=q[:].bitcast(FP8X4), scales=s[:], in_=w_grp[key][:])
 
         prods, a_ps, a_sb, m_bf, m_q, k_ps, k_sb, f_ps, p_bf = {}, {}, {}, {}, {}, {}, {}, {}, {}
         p_q = {}
-        PASSES = ((0, 1, 2), (1, 2))
-        S_PROD = ((0, 0), (0, 2), (1, 0))
 
-        def alloc_prod(u):
-            prods[u] = [work.tile([128, 3, 512], F32, name=f"prod{h}", align_bytes=64) for h in range(2)]
+        def halves(u):
+            return GROUPS[UNITS[u][0]][1] // 128
+
+        def s_prod(u):
+            if u == 0:
+                return ((0, 1), (0, 2), (1, 1))
+            if u < 3:
+                return ()
+            return ((0, 1), (0, 2), (1, 1))
 
         def prod(u, h, i):
-            g, j = divmod(u, J)
-            col = relf[:, 2 * g + h, 3 * j + i : 3 * j + i + 1]
+            if u not in prods:
+                prods[u] = [work.tile([128, 3, 512], F32, name=f"prod{x}", align_bytes=64) for x in range(halves(u))]
+            g, j = UNITS[u]
+            a = GROUPS[g][0] // 128 + h
+            col = relf[:, a, 3 * j + i : 3 * j + i + 1]
             src = w1p[:, i].rearrange("p t q -> p (t q)")
-            if (h, i) in S_PROD:
-                nc.scalar.activation(prods[u][h][:, i, :], src, ACT.Identity, scale=col)
-            elif i not in PASSES[h] or i - 1 in PASSES[h] or i == 0:
-                nc.vector.tensor_scalar(out=prods[u][h][:, i, :], in0=src, scalar1=col, scalar2=None, op0=ALU.mult)
+            dst = prods[u][h][:, i, :]
+            if (h, i) in s_prod(u):
+                nc.scalar.activation(dst, src, ACT.Identity, scale=col)
             else:
-                nc.vector.scalar_tensor_tensor(out=prods[u][h][:, i, :], in0=src, scalar=col, in1=prods[u][h][:, i - 1, :], op0=ALU.mult, op1=ALU.add)
+                nc.vector.tensor_scalar(out=dst, in0=src, scalar1=col, scalar2=None, op0=ALU.mult)
 
         def tr_a(u, tp):
-            bank = psum.tile([128, 2, ROWS], F32, name=f"a_ps{tp}")
+            bank = psum.tile([128, 2, 128 * halves(u)], F32, name=f"a_ps{tp}")
             a_ps.setdefault(u, []).append(bank)
-            for h in range(2):
+            for h in range(halves(u)):
                 for tl in range(2):
                     t = 2 * tp + tl
-                    for i in PASSES[h]:
-                        nc.tensor.matmul(bank[:, tl, h * 128 : (h + 1) * 128], lhsT=prods[u][h][:, i, t * 128 : (t + 1) * 128], rhs=ident[:], start=(i == PASSES[h][0]), stop=(i == 2), is_transpose=True)
+                    for i in range(3):
+                        nc.tensor.matmul(bank[:, tl, h * 128 : (h + 1) * 128], lhsT=prods[u][h][:, i, t * 128 : (t + 1) * 128], rhs=ident[:], start=(i == 0), stop=(i == 2), is_transpose=True)
 
-        def rd_a(u):
-            a_sb[u] = work.tile([128, 4, ROWS], F32, name="a_sb", align_bytes=64)
-            for t in range(4):
-                nc.scalar.activation(a_sb[u][:, t, :], a_ps[u][t // 2][:, t % 2, :], ACT.Identity, bias=b1c[:, t : t + 1])
+        def rd_a(u, tp):
+            if tp == 0:
+                a_sb[u] = work.tile([128, 4, 128 * halves(u)], F32, name="a_sb", align_bytes=64)
+            for tl in range(2):
+                t = 2 * tp + tl
+                nc.scalar.activation(a_sb[u][:, t, :], a_ps[u][tp][:, tl, :], ACT.Identity, bias=b1c[:, t : t + 1])
 
         def leaky(u):
-            m_bf[u] = work.tile([128, ROWS, 4], BF16, name="m_bf", align_bytes=64)
+            m_bf[u] = work.tile([128, 128 * halves(u), 4], BF16, name="m_bf", align_bytes=64)
             a = a_sb[u][:].rearrange("p t r -> p r t")
             nc.vector.scalar_tensor_tensor(out=m_bf[u][:], in0=a, scalar=SLOPE, in1=a, op0=ALU.mult, op1=ALU.max)
 
         def quant_m(u):
-            m_q[u] = (work.tile([128, ROWS], U32, name="m_q", align_bytes=64), work.tile([128, ROWS], U8, name="m_s", align_bytes=64))
+            rows = 128 * halves(u)
+            m_q[u] = (work.tile([128, rows], U32, name="m_q", align_bytes=64), work.tile([128, rows], U8, name="m_s", align_bytes=64))
             nc.vector.quantize_mx(out=m_q[u][0][:].bitcast(FP8X4), scales=m_q[u][1][:], in_=m_bf[u][:].rearrange("p r t -> p (r t)"))
 
         def mx1(u):
             k_ps[u] = []
             for tp in range(2):
-                bank = psum.tile([128, 2, ROWS], F32, name=f"k_ps{tp}")
+                bank = psum.tile([128, 2, 128 * halves(u)], F32, name=f"k_ps{tp}")
                 k_ps[u].append(bank)
                 for tl in range(2):
                     cols = slice((2 * tp + tl) * 128, (2 * tp + tl + 1) * 128)
                     nc.tensor.matmul_mx(bank[:, tl, :], lhsT=w2_q[:, cols].bitcast(FP8X4), lhsT_scale=w2_s[:, cols], rhs=m_q[u][0][:].bitcast(FP8X4), rhs_scale=m_q[u][1][:], start=True, stop=True)
 
         def rd_k(u):
-            k_sb[u] = work.tile([128, 4, ROWS], F32, name="k_sb", align_bytes=64)
+            k_sb[u] = work.tile([128, 4, 128 * halves(u)], F32, name="k_sb", align_bytes=64)
             for t in range(4):
                 nc.scalar.activation(k_sb[u][:, t, :], k_ps[u][t // 2][:, t % 2, :], ACT.Identity, bias=b2c[:, t : t + 1])
 
-        def tr_f(u):
-            g, j = divmod(u, J)
-            f_ps[u] = psum.tile([128, 2, ROWS], F32, name="f_ps", bufs=2)
-            for h in range(2):
-                words = f_sb[2 * g + h][:, j, :].bitcast(F32)
-                for e in range(2):
-                    nc.tensor.transpose(f_ps[u][:, e, h * 128 : (h + 1) * 128], words[:, e : 256 : 2], ident[:])
+        def tr_f(u, part):
+            g, j = UNITS[u]
+            if part == 0:
+                f_ps[u] = psum.tile([128, 2, 128 * halves(u)], F32, name="f_ps", bufs=2)
+            pairs = [(h, e) for h in range(halves(u)) for e in range(2)]
+            for h, e in pairs[: len(pairs) // 2] if part == 0 else pairs[len(pairs) // 2 :]:
+                words = f_sb[GROUPS[g][0] // 128 + h][:, j, :].bitcast(F32)
+                nc.tensor.transpose(f_ps[u][:, e, h * 128 : (h + 1) * 128], words[:, e : 256 : 2], ident[:])
 
-        def times_f(u):
-            p_bf[u] = work.tile([128, ROWS, 4], BF16, name="p_bf", align_bytes=64)
-            fv = f_ps[u][:].rearrange("p u n -> p (u n)").bitcast(BF16).rearrange("p (u n e) -> p n u e", u=2, e=2)
-            kv = k_sb[u][:].rearrange("p (u e) n -> p n u e", e=2)
-            nc.vector.tensor_tensor(out=p_bf[u][:].rearrange("p n (u e) -> p n u e", e=2), in0=fv, in1=kv, op=ALU.mult)
+        def times_f(u, parts):
+            p_bf[u] = work.tile([128, 128 * halves(u), 4], BF16, name="p_bf", align_bytes=64)
+            rows = 128 * halves(u) // parts
+            for x in range(parts):
+                r = slice(x * rows, (x + 1) * rows)
+                for tp in range(2):
+                    fv = f_ps[u][:, tp, r].bitcast(BF16).rearrange("p (n e) -> p n e", e=2)
+                    kv = k_sb[u][:, 2 * tp : 2 * tp + 2, r].rearrange("p e n -> p n e")
+                    nc.vector.tensor_tensor(out=p_bf[u][:, r, 2 * tp : 2 * tp + 2], in0=fv, in1=kv, op=ALU.mult)
 
-        def quant_p(u):
-            g, j = divmod(u, J)
+        def quant_p(u, parts):
+            g, j = UNITS[u]
+            rows = GROUPS[g][1]
             if j == 0:
-                p_q[g] = (work.tile([128, J, ROWS], U32, name="p_q", align_bytes=64), work.tile([128, J, ROWS], U8, name="p_s", align_bytes=64))
-            nc.vector.quantize_mx(out=p_q[g][0][:, j, :].bitcast(FP8X4), scales=p_q[g][1][:, j, :], in_=p_bf[u][:].rearrange("p n t -> p (n t)"))
+                p_q[g] = (work.tile([128, J, rows], U32, name="p_q", align_bytes=64, bufs=3), work.tile([128, J, rows], U8, name="p_s", align_bytes=64, bufs=3))
+            for x in range(parts):
+                r = slice(x * rows // parts, (x + 1) * rows // parts)
+                nc.vector.quantize_mx(out=p_q[g][0][:, j, r].bitcast(FP8X4), scales=p_q[g][1][:, j, r], in_=p_bf[u][:, r, :].rearrange("p n t -> p (n t)"))
 
         o_ps, o_bf, t_ps = {}, {}, {}
         o_q = keep.tile([128, N], U32, name="o_q", align_bytes=64)
         o_s = keep.tile([128, N], U8, name="o_s", align_bytes=64)
 
-        def mx2_planes(a, part):
-            g, h = divmod(a, 2)
-            if part == 0:
+        def group_of(a):
+            g = [x for x in range(len(GROUPS)) if GROUPS[x][0] <= a * 128][-1]
+            r = a * 128 - GROUPS[g][0]
+            return g, slice(r, r + 128)
+
+        def mx2_planes(a, ts):
+            g, rows = group_of(a)
+            if a not in o_ps:
                 o_ps[a] = psum.tile([128, 4, 128], F32, name="o_ps", bufs=2)
-            rows = slice(h * 128, (h + 1) * 128)
-            for t in (0, 1) if part == 0 else (2, 3):
+            for t in ts:
                 cols = slice(t * 128, (t + 1) * 128)
                 for j in range(J):
                     nc.tensor.matmul_mx(o_ps[a][:, t, :], lhsT=wo_q[j][:, cols].bitcast(FP8X4), lhsT_scale=wo_s[j][:, cols], rhs=p_q[g][0][:, j, rows].bitcast(FP8X4), rhs_scale=p_q[g][1][:, j, rows], start=(j == 0), stop=(j == J - 1))
 
-        def mx2_rows(a, part):
-            g, h = divmod(a, 2)
-            if part == 0:
-                t_ps[a] = psum.tile([128, 4, 128], F32, name="o_ps", bufs=2)
-            rows = slice(h * 128, (h + 1) * 128)
-            for j in (0, 1) if part == 0 else (2, 3):
+        def mx2_rows(a, js, tag="o_ps", bufs=2):
+            g, rows = group_of(a)
+            if a not in t_ps:
+                t_ps[a] = psum.tile([128, 4, 128], F32, name=tag, bufs=bufs)
+            for j in js:
                 nc.tensor.matmul_mx(t_ps[a][:].rearrange("n t m -> n (t m)"), lhsT=p_q[g][0][:, j, rows].bitcast(FP8X4), lhsT_scale=p_q[g][1][:, j, rows], rhs=wo_q[j][:].bitcast(FP8X4), rhs_scale=wo_s[j][:], start=(j == 0), stop=(j == J - 1))
 
-        def group_o(a):
+        def group_o(a, eng="v"):
             o_bf[a] = work.tile([128, 128, 4], BF16, name="o_bf", align_bytes=64)
-            nc.vector.tensor_copy(out=o_bf[a][:], in_=o_ps[a][:].rearrange("p t n -> p n t"))
+            src = o_ps[a][:].rearrange("p t n -> p n t")
+            if eng == "v":
+                nc.vector.tensor_copy(out=o_bf[a][:], in_=src)
+            else:
+                nc.scalar.activation(o_bf[a][:], src, ACT.Identity)
 
         def quant_o(a):
             cols = slice(a * 128, (a + 1) * 128)
             nc.vector.quantize_mx(out=o_q[:, cols].bitcast(FP8X4), scales=o_s[:, cols], in_=o_bf[a][:].rearrange("p n t -> p (n t)"))
             nc.sync.dma_start(out=out_1[0, :, cols, :].rearrange("p m t -> p (m t)").bitcast(I32), in_=o_q[:, cols].bitcast(I32))
 
-        def store_scales(c0, c1):
+        def store_scales(c0, c1, queue):
             for q in range(4):
-                nc.sync.dma_start(out=out_2[0, 4 * q : 4 * q + 4, c0:c1].bitcast(I32), in_=o_s[32 * q : 32 * q + 4, c0:c1].bitcast(I32))
+                queue.dma_start(out=out_2[0, 4 * q : 4 * q + 4, c0:c1].bitcast(I32), in_=o_s[32 * q : 32 * q + 4, c0:c1].bitcast(I32))
 
-        def rd_t(a, eng):
+        def rd_t(a, eng="s"):
             r = work.tile([128, 128, 4], F32, name="r_sb", align_bytes=64)
             src = t_ps[a][:].rearrange("n t m -> n m t")
             if eng == "v":
@@ -209,71 +244,131 @@ def tile_rangeviewmetakernelfourneighbour_x1_kernel(tc, rel, w1, b1, w2, b2, f, 
                 nc.scalar.activation(r[:], src, ACT.Identity)
             nc.sync.dma_start(out=out_0[a * 128 : (a + 1) * 128, :], in_=r[:].rearrange("n m t -> n (m t)"))
 
-        fill = {}
-        for q in range(8):
-            g, h = divmod(q, 2)
-            fill[4 * g + 7 + 2 * h] = [("p", q)]
-            fill[4 * g + 8 + 2 * h] = [("r", q)]
-        fill[19], fill[20], fill[21], fill[22] = [("p", 6), ("p", 7)], [("r", 6), ("r", 7)], [], []
+        def stand_in(n):
+            bank = psum.tile([128, 512], F32, name="o_ps", bufs=2)
+            for r in range(n):
+                nc.tensor.matmul_mx(bank[:], lhsT=w2_q[:, 0:128].bitcast(FP8X4), lhsT_scale=w2_s[:, 0:128], rhs=w2_q[:].bitcast(FP8X4), rhs_scale=w2_s[:], start=True, stop=True)
 
-        ok = lambda u: 0 <= u < UNITS
-        mx2 = lambda kq, part: mx2_planes(kq[1], part) if kq[0] == "p" else mx2_rows(kq[1], part)
-        for s in range(22):
-            now = fill.get(s, [])
-            planes = [q for k, q in fill.get(s - 1, []) if k == "p"]
-            rows = [q for k, q in fill.get(s - 1, []) if k == "r"]
+        n_units = len(UNITS)
+        last = n_units - 1
+        ok = lambda u: 0 <= u < n_units
+        queue = []
+        pending_planes, pending_rows = [], []
+        prep = {
+            0: [(1, "i")],
+            1: [(1, "q"), (2, "i")],
+            2: [(2, "q"), (3, "i")],
+            3: [(3, "q")],
+            4: [],
+            5: [],
+            6: [],
+        }
+
+        def do_prep(key, what, scalar_parts=()):
+            raw, q, sc = (w2_raw, w2_q, w2_s) if key == "w2" else (wo_raw[key], wo_q[key], wo_s[key])
+            if what == "i":
+                interleave(key, raw, scalar_parts)
+            else:
+                quant_w(key, q, sc)
+
+        do_prep("w2", "i", (2, 3))
+        do_prep("w2", "q")
+        do_prep(0, "i", (2, 3))
+        do_prep(0, "q")
+        stand_in(6)
+        nc.scalar.activation(b1c[:], b1_raw[:], ACT.Identity)
+        nc.scalar.activation(b2c[:], b2_raw[:], ACT.Identity)
+        nc.vector.tensor_copy(out=relf[:], in_=rel_raw[:])
+        permute("v", 0)
+        permute("s", 1)
+        permute("s", 2)
+        for s in range(n_units + 3):
+            planes, rows = pending_planes, pending_rows
+            pending_planes, pending_rows = [], []
+            now = queue[:1]
+            queue = queue[1:]
             if ok(s - 3):
                 rd_k(s - 3)
-            for q in rows:
-                rd_t(q, "s" if q != 7 else "v")
             if ok(s - 2):
                 leaky(s - 2)
-            if ok(s):
-                alloc_prod(s)
-                prod(s, 1, 0)
-                for i in range(3):
-                    prod(s, 0, i)
-            if ok(s - 2):
-                quant_m(s - 2)
             if ok(s - 1):
                 tr_a(s - 1, 0)
-            for q in now:
-                mx2(q, 0)
+            if ok(s - 2):
+                tr_f(s - 2, 0)
+            todo = [(h, i) for h in range(halves(s)) for i in range(3)] if ok(s) else []
+            for h, i in todo[:3]:
+                prod(s, h, i)
+            if ok(s - 1):
+                rd_a(s - 1, 0)
+            for kind, a in now:
+                if kind == "p":
+                    mx2_planes(a, (0, 1, 2))
+                else:
+                    mx2_rows(a, (0, 1, 2))
+            if ok(s - 1) and not now and 0 < s < 7:
+                stand_in(2)
+            if ok(s - 2):
+                quant_m(s - 2)
+            for h, i in todo[3:5]:
+                prod(s, h, i)
             if ok(s - 1):
                 tr_a(s - 1, 1)
             if ok(s - 2):
-                tr_f(s - 2)
+                tr_f(s - 2, 1)
+            for a in rows:
+                rd_t(a)
+            for a in planes:
+                group_o(a, "s")
+            if ok(s - 3):
+                times_f(s - 3, 2 if s - 3 == last else 1)
+            if ok(s - 2):
                 mx1(s - 2)
-            for q in now:
-                mx2(q, 1)
-            if ok(s):
-                prod(s, 1, 1)
-                prod(s, 1, 2)
+            for kind, a in now:
+                if kind == "p":
+                    mx2_planes(a, (3,))
+                    pending_planes.append(a)
+                else:
+                    mx2_rows(a, (3,))
+                    pending_rows.append(a)
+            if ok(s - 1) and not now and 0 < s < 7:
+                stand_in(0)
+            for h, i in todo[5:]:
+                prod(s, h, i)
             if ok(s - 3):
-                times_f(s - 3)
-            for q in planes:
-                group_o(q)
+                quant_p(s - 3, 2 if s - 3 == last else 1)
+                g, j = UNITS[s - 3]
+                if j == J - 1 and s - 3 < last:
+                    for a in range(GROUPS[g][0] // 128, (GROUPS[g][0] + GROUPS[g][1]) // 128):
+                        queue += [("p", a), ("r", a)]
+            for a in planes:
+                quant_o(a)
             if ok(s - 1):
-                rd_a(s - 1)
-            if ok(s - 3):
-                quant_p(s - 3)
-            for q in planes:
-                quant_o(q)
+                rd_a(s - 1, 1)
+            if s == last + 2:
+                mx2_rows(6, (0, 1), "a_ps0", 1)
+                mx2_rows(7, (0, 1), "a_ps1", 1)
+            if s == last + 3:
+                mx2_rows(6, (2,))
+                mx2_rows(7, (2,))
+            for p in prep.get(s, ()):
+                do_prep(*p)
             if s == 0:
-                interleave("w2", w2_raw, "v")
-                quant_w("w2", w2_q, w2_s)
-            if s == 1:
-                interleave(0, wo_raw[0], "s")
-                interleave(2, wo_raw[2], "v")
-            if s == 2:
-                quant_w(0, wo_q[0], wo_s[0])
-                quant_w(2, wo_q[2], wo_s[2])
-                interleave(1, wo_raw[1], "s")
-                interleave(3, wo_raw[3], "v")
-            if s == 3:
-                quant_w(1, wo_q[1], wo_s[1])
-                quant_w(3, wo_q[3], wo_s[3])
-            if s == 18:
-                store_scales(0, 768)
-            if s == 20:
-                store_scales(768, 1024)
+                stand_in(0)
+            if s == last:
+                store_scales(0, 512, nc.sync)
+        for a in pending_planes:
+            group_o(a)
+            quant_o(a)
+        for a in pending_rows:
+            rd_t(a)
+        mx2_planes(6, (0, 1, 2, 3))
+        mx2_planes(7, (0, 1, 2, 3))
+        mx2_rows(6, (3,))
+        mx2_rows(7, (3,))
+        group_o(6, "s")
+        group_o(7)
+        rd_t(6)
+        rd_t(7, "s")
+        quant_o(6)
+        quant_o(7)
+        store_scales(512, 1024, nc.scalar)

from contextlib import ExitStack

import concourse.mybir as mybir
from concourse.masks import make_identity

F32 = mybir.dt.float32
BF16 = mybir.dt.bfloat16
U32 = mybir.dt.uint32
I32 = mybir.dt.int32
U8 = mybir.dt.uint8
FP8X4 = mybir.dt.float8_e4m3fn_x4
ALU = mybir.AluOpType
ACT = mybir.ActivationFunctionType

N, J, H, C, O = 1024, 4, 512, 512, 512
FLOPS = 2 * N * J * H * C + 2 * N * J * C * O
GROUPS = [(0, 256), (256, 256), (512, 256), (768, 256)]
UNITS = [(g, j) for g in range(len(GROUPS)) for j in range(J)]
SLOPE = 0.2


def tile_rangeviewmetakernelfourneighbour_x1_kernel(tc, rel, w1, b1, w2, b2, f, wo, out_0, out_1, out_2):
    nc = tc.nc
    with ExitStack() as ctx:
        keep = ctx.enter_context(tc.tile_pool(name="keep", bufs=1))
        work = ctx.enter_context(tc.tile_pool(name="work", bufs=2))
        psum = ctx.enter_context(tc.psum_pool(name="psum", bufs=1))
        ctx.enter_context(tc.manual_schedule())

        w2_raw = keep.tile([128, 4, 512], BF16, name="w2_raw")
        rel_raw = keep.tile([128, 8, 12], BF16, name="rel_raw")
        w1_raw = keep.tile([128, 3, 512], BF16, name="w1_raw")
        b1_raw = keep.tile([128, 4], BF16, name="b1_raw")
        b2_raw = keep.tile([128, 4], BF16, name="b2_raw")
        wo_raw = [keep.tile([128, 4, 512], BF16, name=f"wo_raw{j}") for j in range(J)]
        f_sb = [keep.tile([128, J, 512], BF16, name=f"f_sb{a}") for a in range(8)]

        def load_w2():
            nc.sync.dma_start(out=w2_raw[:], in_=w2.rearrange("(p k) c -> p k c", k=4))

        def load_rel():
            nc.sync.dma_start(out=rel_raw[:], in_=rel.rearrange("(a p) j i -> p a (j i)", p=128))
            nc.sync.dma_start(out=b1_raw[:], in_=b1.rearrange("(p t) -> p t", t=4))
            nc.sync.dma_start(out=b2_raw[:], in_=b2.rearrange("(p t) -> p t", t=4))

        def load_w1():
            nc.sync.dma_start(out=w1_raw[:], in_=w1.partition_broadcast(128))

        def load_wo(j):
            nc.sync.dma_start(out=wo_raw[j][:], in_=wo[j].rearrange("(p k) c -> p k c", k=4))

        def load_f(a):
            nc.sync.dma_start(out=f_sb[a][:], in_=f[a * 128 : (a + 1) * 128])

        load_w2()
        load_wo(0)
        load_rel()
        load_w1()
        load_wo(1)
        load_wo(2)
        load_f(0)
        load_f(1)
        load_wo(3)
        for a in range(2, 8):
            load_f(a)

        ident = keep.tile([128, 128], F32, name="ident")
        make_identity(nc, ident[:])

        b1c = keep.tile([128, 4], F32, name="b1c")
        b2c = keep.tile([128, 4], F32, name="b2c")
        relf = keep.tile([128, 8, 12], F32, name="relf")
        w1p = keep.tile([128, 3, 4, 128], BF16, name="w1p")

        def permute(eng, i):
            v = w1_raw[:, i, :].rearrange("p (q t) -> p t q", t=4)
            if eng == "v":
                nc.vector.tensor_copy(out=w1p[:, i], in_=v)
            else:
                nc.scalar.copy(w1p[:, i], v)

        w2_q = keep.tile([128, 512], U32, name="w2_q", align_bytes=64)
        w2_s = keep.tile([128, 512], U8, name="w2_s", align_bytes=64)
        wo_q = [keep.tile([128, 512], U32, name=f"wo_q{j}", align_bytes=64) for j in range(J)]
        wo_s = [keep.tile([128, 512], U8, name=f"wo_s{j}", align_bytes=64) for j in range(J)]
        w_grp = {}

        def interleave(key, raw, on_scalar, parts=(0, 1, 2, 3)):
            if key not in w_grp:
                w_grp[key] = work.tile([128, 2048], BF16, name="w_grp", align_bytes=64, bufs=4)
            dst = w_grp[key][:].rearrange("p (t m k) -> p t m k", t=4, k=4)
            src = raw[:].rearrange("p k (m t) -> p t m k", t=4)
            for t in parts:
                if t in on_scalar:
                    nc.scalar.copy(dst[:, t], src[:, t])
                else:
                    nc.vector.tensor_copy(out=dst[:, t], in_=src[:, t])

        def quant_w(key, q, s):
            nc.vector.quantize_mx(out=q[:].bitcast(FP8X4), scales=s[:], in_=w_grp[key][:])

        prods, a_ps, a_sb, m_bf, m_q, k_ps, k_sb, f_ps, p_bf = {}, {}, {}, {}, {}, {}, {}, {}, {}
        p_q = {}

        def halves(u):
            return GROUPS[UNITS[u][0]][1] // 128

        def s_prod(u):
            if u == 0:
                return ((0, 1), (0, 2), (1, 1))
            if u < 3:
                return ()
            return ((0, 1), (0, 2), (1, 1))

        def prod(u, h, i):
            if u not in prods:
                prods[u] = [work.tile([128, 3, 512], F32, name=f"prod{x}", align_bytes=64) for x in range(halves(u))]
            g, j = UNITS[u]
            a = GROUPS[g][0] // 128 + h
            col = relf[:, a, 3 * j + i : 3 * j + i + 1]
            src = w1p[:, i].rearrange("p t q -> p (t q)")
            dst = prods[u][h][:, i, :]
            if (h, i) in s_prod(u):
                nc.scalar.activation(dst, src, ACT.Identity, scale=col)
            else:
                nc.vector.tensor_scalar(out=dst, in0=src, scalar1=col, scalar2=None, op0=ALU.mult)

        def tr_a(u, tp):
            bank = psum.tile([128, 2, 128 * halves(u)], F32, name=f"a_ps{tp}")
            a_ps.setdefault(u, []).append(bank)
            for h in range(halves(u)):
                for tl in range(2):
                    t = 2 * tp + tl
                    for i in range(3):
                        nc.tensor.matmul(bank[:, tl, h * 128 : (h + 1) * 128], lhsT=prods[u][h][:, i, t * 128 : (t + 1) * 128], rhs=ident[:], start=(i == 0), stop=(i == 2), is_transpose=True)

        def rd_a(u, tp):
            if tp == 0:
                a_sb[u] = work.tile([128, 4, 128 * halves(u)], F32, name="a_sb", align_bytes=64)
            for tl in range(2):
                t = 2 * tp + tl
                nc.scalar.activation(a_sb[u][:, t, :], a_ps[u][tp][:, tl, :], ACT.Identity, bias=b1c[:, t : t + 1])

        def leaky(u):
            m_bf[u] = work.tile([128, 128 * halves(u), 4], BF16, name="m_bf", align_bytes=64)
            a = a_sb[u][:].rearrange("p t r -> p r t")
            nc.vector.scalar_tensor_tensor(out=m_bf[u][:], in0=a, scalar=SLOPE, in1=a, op0=ALU.mult, op1=ALU.max)

        def quant_m(u):
            rows = 128 * halves(u)
            m_q[u] = (work.tile([128, rows], U32, name="m_q", align_bytes=64), work.tile([128, rows], U8, name="m_s", align_bytes=64))
            nc.vector.quantize_mx(out=m_q[u][0][:].bitcast(FP8X4), scales=m_q[u][1][:], in_=m_bf[u][:].rearrange("p r t -> p (r t)"))

        def mx1(u):
            k_ps[u] = []
            for tp in range(2):
                bank = psum.tile([128, 2, 128 * halves(u)], F32, name=f"k_ps{tp}")
                k_ps[u].append(bank)
                for tl in range(2):
                    cols = slice((2 * tp + tl) * 128, (2 * tp + tl + 1) * 128)
                    nc.tensor.matmul_mx(bank[:, tl, :], lhsT=w2_q[:, cols].bitcast(FP8X4), lhsT_scale=w2_s[:, cols], rhs=m_q[u][0][:].bitcast(FP8X4), rhs_scale=m_q[u][1][:], start=True, stop=True)

        def rd_k(u):
            k_sb[u] = work.tile([128, 4, 128 * halves(u)], F32, name="k_sb", align_bytes=64)
            for t in range(4):
                nc.scalar.activation(k_sb[u][:, t, :], k_ps[u][t // 2][:, t % 2, :], ACT.Identity, bias=b2c[:, t : t + 1])

        def tr_f(u, part):
            g, j = UNITS[u]
            if part == 0:
                f_ps[u] = psum.tile([128, 2, 128 * halves(u)], F32, name="f_ps", bufs=2)
            pairs = [(h, e) for h in range(halves(u)) for e in range(2)]
            for h, e in pairs[: len(pairs) // 2] if part == 0 else pairs[len(pairs) // 2 :]:
                words = f_sb[GROUPS[g][0] // 128 + h][:, j, :].bitcast(F32)
                nc.tensor.transpose(f_ps[u][:, e, h * 128 : (h + 1) * 128], words[:, e : 256 : 2], ident[:])

        def times_f(u, parts):
            p_bf[u] = work.tile([128, 128 * halves(u), 4], BF16, name="p_bf", align_bytes=64)
            rows = 128 * halves(u) // parts
            for x in range(parts):
                r = slice(x * rows, (x + 1) * rows)
                for tp in range(2):
                    fv = f_ps[u][:, tp, r].bitcast(BF16).rearrange("p (n e) -> p n e", e=2)
                    kv = k_sb[u][:, 2 * tp : 2 * tp + 2, r].rearrange("p e n -> p n e")
                    nc.vector.tensor_tensor(out=p_bf[u][:, r, 2 * tp : 2 * tp + 2], in0=fv, in1=kv, op=ALU.mult)

        def quant_p(u, parts):
            g, j = UNITS[u]
            rows = GROUPS[g][1]
            if j == 0:
                p_q[g] = (work.tile([128, J, rows], U32, name="p_q", align_bytes=64, bufs=3), work.tile([128, J, rows], U8, name="p_s", align_bytes=64, bufs=3))
            for x in range(parts):
                r = slice(x * rows // parts, (x + 1) * rows // parts)
                nc.vector.quantize_mx(out=p_q[g][0][:, j, r].bitcast(FP8X4), scales=p_q[g][1][:, j, r], in_=p_bf[u][:, r, :].rearrange("p n t -> p (n t)"))

        o_ps, o_bf, t_ps = {}, {}, {}
        o_q = keep.tile([128, N], U32, name="o_q", align_bytes=64)
        o_s = keep.tile([128, N], U8, name="o_s", align_bytes=64)

        def group_of(a):
            g = [x for x in range(len(GROUPS)) if GROUPS[x][0] <= a * 128][-1]
            r = a * 128 - GROUPS[g][0]
            return g, slice(r, r + 128)

        def mx2_planes(a, ts):
            g, rows = group_of(a)
            if a not in o_ps:
                o_ps[a] = psum.tile([128, 4, 128], F32, name="o_ps", bufs=2)
            for t in ts:
                cols = slice(t * 128, (t + 1) * 128)
                for j in range(J):
                    nc.tensor.matmul_mx(o_ps[a][:, t, :], lhsT=wo_q[j][:, cols].bitcast(FP8X4), lhsT_scale=wo_s[j][:, cols], rhs=p_q[g][0][:, j, rows].bitcast(FP8X4), rhs_scale=p_q[g][1][:, j, rows], start=(j == 0), stop=(j == J - 1))

        def mx2_rows(a, js, tag="o_ps", bufs=2):
            g, rows = group_of(a)
            if a not in t_ps:
                t_ps[a] = psum.tile([128, 4, 128], F32, name=tag, bufs=bufs)
            for j in js:
                nc.tensor.matmul_mx(t_ps[a][:].rearrange("n t m -> n (t m)"), lhsT=p_q[g][0][:, j, rows].bitcast(FP8X4), lhsT_scale=p_q[g][1][:, j, rows], rhs=wo_q[j][:].bitcast(FP8X4), rhs_scale=wo_s[j][:], start=(j == 0), stop=(j == J - 1))

        def group_o(a, eng="v"):
            o_bf[a] = work.tile([128, 128, 4], BF16, name="o_bf", align_bytes=64)
            src = o_ps[a][:].rearrange("p t n -> p n t")
            if eng == "v":
                nc.vector.tensor_copy(out=o_bf[a][:], in_=src)
            else:
                nc.scalar.activation(o_bf[a][:], src, ACT.Identity)

        def quant_o(a):
            cols = slice(a * 128, (a + 1) * 128)
            nc.vector.quantize_mx(out=o_q[:, cols].bitcast(FP8X4), scales=o_s[:, cols], in_=o_bf[a][:].rearrange("p n t -> p (n t)"))
            nc.sync.dma_start(out=out_1[0, :, cols, :].rearrange("p m t -> p (m t)").bitcast(I32), in_=o_q[:, cols].bitcast(I32))

        def store_scales(c0, c1, queue):
            for q in range(4):
                queue.dma_start(out=out_2[0, 4 * q : 4 * q + 4, c0:c1].bitcast(I32), in_=o_s[32 * q : 32 * q + 4, c0:c1].bitcast(I32))

        def rd_t(a, eng="s"):
            r = work.tile([128, 128, 4], F32, name="r_sb", align_bytes=64)
            src = t_ps[a][:].rearrange("n t m -> n m t")
            if eng == "v":
                nc.vector.tensor_copy(out=r[:], in_=src)
            else:
                nc.scalar.activation(r[:], src, ACT.Identity)
            nc.sync.dma_start(out=out_0[a * 128 : (a + 1) * 128, :], in_=r[:].rearrange("n m t -> n (m t)"))

        def stand_in(n):
            bank = psum.tile([128, 512], F32, name="o_ps", bufs=2)
            for r in range(n):
                nc.tensor.matmul_mx(bank[:], lhsT=w2_q[:, 0:128].bitcast(FP8X4), lhsT_scale=w2_s[:, 0:128], rhs=w2_q[:].bitcast(FP8X4), rhs_scale=w2_s[:], start=True, stop=True)

        n_units = len(UNITS)
        last = n_units - 1
        ok = lambda u: 0 <= u < n_units
        queue = []
        pending_planes, pending_rows = [], []
        prep = {
            0: [(1, "i")],
            1: [(1, "q"), (2, "i")],
            2: [(2, "q"), (3, "i")],
            3: [(3, "q")],
            4: [],
            5: [],
            6: [],
        }

        def do_prep(key, what, scalar_parts=()):
            raw, q, sc = (w2_raw, w2_q, w2_s) if key == "w2" else (wo_raw[key], wo_q[key], wo_s[key])
            if what == "i":
                interleave(key, raw, scalar_parts)
            else:
                quant_w(key, q, sc)

        do_prep("w2", "i", (2, 3))
        do_prep("w2", "q")
        do_prep(0, "i", (2, 3))
        do_prep(0, "q")
        stand_in(6)
        nc.scalar.activation(b1c[:], b1_raw[:], ACT.Identity)
        nc.scalar.activation(b2c[:], b2_raw[:], ACT.Identity)
        nc.vector.tensor_copy(out=relf[:], in_=rel_raw[:])
        permute("v", 0)
        permute("s", 1)
        permute("s", 2)
        for s in range(n_units + 3):
            planes, rows = pending_planes, pending_rows
            pending_planes, pending_rows = [], []
            now = queue[:1]
            queue = queue[1:]
            if ok(s - 3):
                rd_k(s - 3)
            if ok(s - 2):
                leaky(s - 2)
            if ok(s - 1):
                tr_a(s - 1, 0)
            if ok(s - 2):
                tr_f(s - 2, 0)
            todo = [(h, i) for h in range(halves(s)) for i in range(3)] if ok(s) else []
            for h, i in todo[:3]:
                prod(s, h, i)
            if ok(s - 1):
                rd_a(s - 1, 0)
            for kind, a in now:
                if kind == "p":
                    mx2_planes(a, (0, 1, 2))
                else:
                    mx2_rows(a, (0, 1, 2))
            if ok(s - 1) and not now and 0 < s < 7:
                stand_in(2)
            if ok(s - 2):
                quant_m(s - 2)
            for h, i in todo[3:5]:
                prod(s, h, i)
            if ok(s - 1):
                tr_a(s - 1, 1)
            if ok(s - 2):
                tr_f(s - 2, 1)
            for a in rows:
                rd_t(a)
            for a in planes:
                group_o(a, "s")
            if ok(s - 3):
                times_f(s - 3, 2 if s - 3 == last else 1)
            if ok(s - 2):
                mx1(s - 2)
            for kind, a in now:
                if kind == "p":
                    mx2_planes(a, (3,))
                    pending_planes.append(a)
                else:
                    mx2_rows(a, (3,))
                    pending_rows.append(a)
            if ok(s - 1) and not now and 0 < s < 7:
                stand_in(0)
            for h, i in todo[5:]:
                prod(s, h, i)
            if ok(s - 3):
                quant_p(s - 3, 2 if s - 3 == last else 1)
                g, j = UNITS[s - 3]
                if j == J - 1 and s - 3 < last:
                    for a in range(GROUPS[g][0] // 128, (GROUPS[g][0] + GROUPS[g][1]) // 128):
                        queue += [("p", a), ("r", a)]
            for a in planes:
                quant_o(a)
            if ok(s - 1):
                rd_a(s - 1, 1)
            if s == last + 2:
                mx2_rows(6, (0, 1), "a_ps0", 1)
                mx2_rows(7, (0, 1), "a_ps1", 1)
            if s == last + 3:
                mx2_rows(6, (2,))
                mx2_rows(7, (2,))
            for p in prep.get(s, ()):
                do_prep(*p)
            if s == 0:
                stand_in(0)
            if s == last:
                store_scales(0, 512, nc.sync)
        for a in pending_planes:
            group_o(a)
            quant_o(a)
        for a in pending_rows:
            rd_t(a)
        mx2_planes(6, (0, 1, 2, 3))
        mx2_planes(7, (0, 1, 2, 3))
        mx2_rows(6, (3,))
        mx2_rows(7, (3,))
        group_o(6, "s")
        group_o(7)
        rd_t(6)
        rd_t(7, "s")
        quant_o(6)
        quant_o(7)
        store_scales(512, 1024, nc.scalar)
